import numpy as np, ml_dtypes
CORES = [2,3,42,43,82,83,122,123]
N = 8
import mx_ref
NC, G, S2 = 192, 4, 7
C = np.float32(0.047)
CNT = [[0,28,12,52,44,32,0,24],[12,32,56,4,0,52,12,24],[12,12,36,0,20,28,52,32],[36,0,36,32,0,0,20,68],[72,0,0,44,0,16,28,32],[24,52,0,12,36,52,4,12],[36,64,52,0,28,12,0,0],[0,4,0,48,64,0,76,0]]
OFF = [[sum(c[:e]) for e in range(N + 1)] for c in CNT]
BF = ml_dtypes.bfloat16
def cut(t, i, w=512):
    return t[:, w * i:w * i + w]
def tile(rs):
    return np.stack(rs, axis=2).reshape(128, -1).astype(BF)
def layer(w, X):
    out = []
    for i in range(G):
        for t in range(len(X)):
            p = mx_ref.matmul(mx_ref.quantize(cut(w, len(X) * i + t)), X[t])
            z = p if t == 0 else z + p
        out.append(z)
    return out
def act(Z):
    return [np.maximum(z, 0) * C for z in Z]
def setup_inputs(rng):
    def f(*shape):
        return mx_ref.flush((rng.standard_normal(shape, dtype=np.float32) * np.exp2(rng.integers(-2, 3, shape[:-1] + (1,)))).astype(BF))
    gt = (0.125 + 0.875 * rng.random((N, 2, NC))).astype(BF)
    return {"gt": gt, "x": f(N, 128, 4 * NC), "w1": f(N, 128, G * 512), "w2": f(N, 128, 512)}
def setup_inputs_blocks(rng):
    d = setup_inputs(rng)
    for k in ("x", "w1", "w2"): d[k] = mx_ref.spread(d[k], rng, 4)
    return d
def setup_inputs_wide(rng):
    d = setup_inputs(rng)
    for k in ("x", "w1", "w2"): d[k] = mx_ref.flush((d[k].astype(np.float32) * np.exp2(rng.integers(-8, 9, (N, 1, 1))).astype(np.float32)).astype(BF))
    return d
def setup_inputs_zeros(rng):
    d = setup_inputs(rng); v = d["x"].reshape(N, 128, -1, 4).copy()
    v[np.broadcast_to((rng.random((N, 1, v.shape[2], 1)) < 0.33), v.shape)] = 0
    d["x"] = v.reshape(d["x"].shape)
    return d
def reference(gt, x, w1, w2):
    y = np.zeros((N, 128, NC), np.float32); g = gt.astype(np.float32)
    for e in range(N):
        f = (e - S2) % N
        t = np.concatenate([x[j][:, 4 * OFF[j][k]:4 * OFF[j][k + 1]] for k in (e, f) for j in range(N)], axis=1)
        p = mx_ref.matmul(mx_ref.quantize(w2[e]), mx_ref.quantize(tile(act(layer(w1[e], [mx_ref.quantize(t)])))))
        c = 0
        for i, k in enumerate((e, f)):
            for j in range(N):
                a, b = OFF[j][k], OFF[j][k + 1]
                y[j][:, a:b] = y[j][:, a:b] + p[:, c:c + b - a] * g[j, i, a:b]; c += b - a
    return {"y": y}

@@ -1,0 +1,349 @@
+from concourse.bass import DstId, RemoteDMATransfer
+from concourse.mybir import dt, AluOpType, ActivationFunctionType
+
+N, NC, G = 8, 192, 4
+KC = 0.047
+XE = 272
+LD = 288
+
+SCRATCH = {
+    "xt": ("sbuf", [128, 4 * XE], "bfloat16"),
+    "w1t": ("sbuf", [128, 2048], "bfloat16"),
+    "w2t": ("sbuf", [128, 512], "bfloat16"),
+    "qx": ("sbuf", [128, XE], "float8_e4m3fn_x4"),
+    "sx": ("sbuf", [128, XE], "uint8"),
+    "ql": ("sbuf", [128, LD], "float8_e4m3fn_x4"),
+    "sl": ("sbuf", [128, LD], "uint8"),
+    "qw0": ("sbuf", [128, 640], "float8_e4m3fn_x4"),
+    "sw0": ("sbuf", [128, 640], "uint8"),
+    "qw1": ("sbuf", [128, 640], "float8_e4m3fn_x4"),
+    "sw1": ("sbuf", [128, 640], "uint8"),
+    "pof": ("sbuf", [128, 128], "float32"),
+    "res": ("sbuf", [128, LD], "float32"),
+    "two": ("sbuf", [128, LD + 128], "float32"),
+    "gst": ("dram", [128, 4], "bfloat16"),
+    "gl": ("dram", [3, 128, 4], "bfloat16"),
+    "grow": ("sbuf", [128, 640], "bfloat16"),
+    "gb": ("sbuf", [128, 640], "bfloat16"),
+    "y0": ("sbuf", [128, NC + 128], "float32"),
+    "y1": ("sbuf", [128, NC + 128], "float32"),
+    "yf": ("sbuf", [128, NC], "float32"),
+    "ps": ("psum", [128, 4096], "float32"),
+}
+PASS = ("of", "f", "l", "ol")
+for _n, _w in zip(PASS, (128, LD, LD, 128)):
+    SCRATCH["h" + _n] = ("sbuf", [128, 4 * _w], "bfloat16")
+    SCRATCH["qh" + _n] = ("sbuf", [128, _w], "float8_e4m3fn_x4")
+    SCRATCH["sh" + _n] = ("sbuf", [128, _w], "uint8")
+SEMAPHORES = (["lx", "lg", "lw1a", "lw1b", "lw2", "mz", "qx_", "qwa", "qwb", "qw2", "ga", "gr", "gbd", "xa", "wa", "ra", "ls",
+               "add", "yd", "pofc", "tf", "to", "outo", "mo"]
+              + [c + n + str(b) for c in "zr" for n in PASS for b in range(G)] + [c + n for c in "qp" for n in PASS]
+              + [c + str(s) for c in "mo" for s in range(3)])
+
+
+def rank_program(g, core, T, topo):
+    me = T.rank_of(core)
+    if me is None:
+        return
+    S = T.sem
+    cnt = T.tables["CNT"]
+    off = [[sum(c[:e]) for e in range(N + 1)] for c in cnt]
+    chips = []
+    for r in range(N):
+        c = topo.chip(T.cores[r])
+        if c not in chips:
+            chips.append(c)
+    grp = [[r for r in range(N) if topo.chip(T.cores[r]) == c] for c in chips]
+    K = len(grp)
+
+    def place(r):
+        for k in range(K):
+            if r in grp[k]:
+                return k, grp[k].index(r)
+
+    def abc(j, k):
+        lo, hi = grp[k]
+        return cnt[j][lo], cnt[j][hi], cnt[j][(hi + 1) % N]
+
+    def xplan(j):
+        k, _ = place(j)
+        s0 = (grp[k][1] + 1) % N
+        pos = [0]
+        for i in range(N + 1):
+            pos.append(pos[-1] + cnt[j][(s0 + i) % N])
+        start = {}
+        for m in range(K):
+            start[m] = pos[(grp[m][0] - s0) % N]
+        return s0, pos[-1], start
+
+    def sources(r):
+        k, p = place(r)
+        o = [grp[m][p] for m in range(K) if m != k]
+        tot = sum(sum(abc(s, k)) for s in o)
+        best = None
+        for i in range(3):
+            for l in range(3):
+                if i != l and tot - abc(o[i], k)[0] >= 128 and tot - abc(o[l], k)[2] >= 128:
+                    v = abc(o[i], k)[0] + abc(o[l], k)[2]
+                    if best is None or v > best[0]:
+                        best = (v, [o[i], o[3 - i - l], o[l]])
+        return best[1]
+
+    def landing(r):
+        k, _ = place(r)
+        c = 0
+        out = {}
+        for s in sources(r):
+            out[s] = c
+            c += sum(abc(s, k))
+        return out, c
+
+    k, p = place(me)
+    lo, hi = grp[k]
+    mate = grp[k][1 - p]
+    peers = [grp[(k + d) % K][p] for d in range(1, K)]
+    srcs = sources(me)
+    land, end = landing(me)
+    s0, E, start = xplan(me)
+    far = topo.mask(core, T.cores[peers[0]])
+    near = topo.mask(core, T.cores[mate])
+    for q in peers:
+        far = far & topo.mask(core, T.cores[q])
+    near = near & ~far
+
+    def bits(m):
+        return bin(m).count("1")
+
+    sent = [0]
+
+    def put(dst, out, in_, sem, mask):
+        rid, pid, _ = topo.addr(T.cores[dst])
+        g.remote_dma(out, in_, sem, S.ls, pid, rid, mask)
+        sent[0] += bits(mask)
+
+    n1 = NC - off[me][s0]
+    gr0 = 2 * NC // 4
+    g.scalar.dma_start(T.gst[0:gr0, :], T.gt[:]).then_inc(S.lg, 16)
+    g.sync.dma_start(T.xt[:, 0:4 * n1], T.x[:, 4 * off[me][s0]:4 * NC]).then_inc(S.lx, 16)
+    nlx = 16
+    if E > n1:
+        g.scalar.dma_start(T.xt[:, 4 * n1:4 * E], T.x[:, 0:4 * (E - n1)]).then_inc(S.lx, 16)
+        nlx = 32
+    g.scalar.dma_start(T.gst[gr0:128, :], T.gt[0:1, 0:4 * (128 - gr0)]).then_inc(S.lg, 16)
+    g.sync.dma_start(T.w1t[:, 0:1024], T.w1[:, 0:1024]).then_inc(S.lw1a, 16)
+    g.scalar.dma_start(T.w1t[:, 1024:2048], T.w1[:, 1024:2048]).then_inc(S.lw1b, 16)
+    g.sync.dma_start(T.w2t[:], T.w2[:]).then_inc(S.lw2, 16)
+
+    grow = {}
+    c = 0
+    loads = []
+    for s in srcs + [me]:
+        o = off[s]
+        a, b, cc = abc(s, k)
+        e2 = (hi + 1) % N
+        grow[s] = (c, c + a + b)
+        for row, at, n in ((0, o[lo], a), (1, o[hi], b), (0, o[hi], b), (1, o[e2], cc)):
+            if n:
+                loads.append((s, row, at, n, c))
+            c += n
+    ng = c
+    for s, row, at, n, c in loads:
+        if s == me:
+            g.sync.dma_start(T.grow[0:1, c:c + n], T.gt[row:row + 1, at:at + n]).then_inc(S.gr, 16)
+    g.sync.wait_ge(S.ga, 3 * bits(far))
+    for s, row, at, n, c in loads:
+        if s != me:
+            r0 = (row * NC + at) // 4
+            g.sync.dma_start(T.grow[0:1, c:c + n], T.gl[srcs.index(s)][r0:r0 + n // 4, :]).then_inc(S.gr, 16)
+
+    g.wait_ge(S.lg, 32)
+    ids, dsts = [], []
+    for q in peers:
+        rid, pid, _ = topo.addr(T.cores[q])
+        ids.append(DstId(rid=rid, pnc=pid))
+        dsts.append(T.gl[sources(q).index(me)])
+    g.remote_dma_fused([RemoteDMATransfer(dst_ids=ids, dma_engine_mask=far, remote_sem=S.ga,
+                                          srcs=[T.gst[:]], dsts=dsts, alu_op=0)], local_sem=S.ls)
+    sent[0] += bits(far)
+    g.wait_ge(S.qx_, 1)
+    for q in peers:
+        kq = place(q)[0]
+        a, n = start[kq], sum(abc(me, kq))
+        d = landing(q)[0][me]
+        put(q, T.ql[:, d:d + n].bitcast(dt.uint8), T.qx[:, a:a + n].bitcast(dt.uint8), S.xa, far)
+        put(q, T.sl[:, d:d + n], T.sx[:, a:a + n], S.xa, far)
+    g.wait_ge(S.qwa, 1)
+    g.wait_ge(S.qwb, 1)
+    g.wait_ge(S.qw2, 1)
+    put(mate, T.qw1[:].bitcast(dt.uint8), T.qw0[:].bitcast(dt.uint8), S.wa, near)
+    put(mate, T.sw1[:], T.sw0[:], S.wa, near)
+    g.wait_ge(S.gr, 16 * len(loads))
+    g.partition_broadcast(T.gb[:, 0:ng], T.grow[0:1, 0:ng], 128).then_inc(S.gbd, 1)
+
+    A0, C0 = abc(srcs[0], k)[0], abc(srcs[-1], k)[2]
+    wlo, whi = (0, end - C0), (A0, end)
+    wf, wl = (wlo, whi) if p == 0 else (whi, wlo)
+    wo = (E - 128, E)
+    no = sum(abc(me, k))
+    oc = 128 - no
+    wins = {"of": wo, "f": wf, "l": wl, "ol": wo}
+    banks = {"of": (4, 5, 6, 7), "f": (0, 1, 2, 3), "l": (4, 5, 6, 7), "ol": (1, 2, 3, 5)}
+    PB = {"of": 4, "f": 0, "l": 4, "ol": 6}
+    BANK = 512
+
+    def bank(b, n):
+        return T.ps[:, BANK * b:BANK * b + n]
+
+    def width(name):
+        return wins[name][1] - wins[name][0]
+
+    def zs(name, qw, sw, qm, sm):
+        u, v = wins[name]
+        for b in range(G):
+            g.tensor.matmul_mx(bank(banks[name][b], v - u), qw[:, 128 * b:128 * b + 128], sw[:, 128 * b:128 * b + 128],
+                               qm[:, u:v], sm[:, u:v], True, True).then_inc(S["z%s%d" % (name, b)], 1)
+
+    def ptile(name, qw, sw):
+        n = width(name)
+        g.tensor.wait_ge(S["q" + name], 1)
+        g.tensor.matmul_mx(bank(PB[name], n), qw[:, 512:640], sw[:, 512:640], T["qh" + name][:, 0:n], T["sh" + name][:, 0:n],
+                           True, True).then_inc(S["p" + name], 1)
+
+    g.tensor.wait_ge(S.qx_, 1)
+    g.tensor.wait_ge(S.qwa, 1)
+    g.tensor.wait_ge(S.qwb, 1)
+    zs("of", T.qw0, T.sw0, T.qx, T.sx)
+    g.tensor.wait_ge(S.qw2, 1)
+    ptile("of", T.qw0, T.sw0)
+    g.tensor.wait_ge(S.xa, 6 * bits(far))
+    zs("f", T.qw0, T.sw0, T.ql, T.sl)
+    g.tensor.wait_ge(S.wa, 2 * bits(near))
+    g.tensor.wait_ge(S.pofc, 1)
+    zs("l", T.qw1, T.sw1, T.ql, T.sl)
+    ptile("f", T.qw0, T.sw0)
+    ptile("l", T.qw1, T.sw1)
+    zs("ol", T.qw1, T.sw1, T.qx, T.sx)
+    ptile("ol", T.qw1, T.sw1)
+
+    def relu_s(name, b):
+        n = width(name)
+        g.scalar.wait_ge(S["z%s%d" % (name, b)], 1)
+        g.scalar.activation(T["h" + name][:, b:4 * n:4], bank(banks[name][b], n), ActivationFunctionType.Relu,
+                            scale=KC).then_inc(S["r%s%d" % (name, b)], 1)
+
+    def relu_v(name, b):
+        n = width(name)
+        g.vector.wait_ge(S["z%s%d" % (name, b)], 1)
+        g.vector.tensor_scalar(T["h" + name][:, b:4 * n:4], bank(banks[name][b], n), 0.0, KC, AluOpType.max,
+                               AluOpType.mult).then_inc(S["r%s%d" % (name, b)], 1)
+
+    def quant(name):
+        n = width(name)
+        for b in range(G):
+            g.vector.wait_ge(S["r%s%d" % (name, b)], 1)
+        g.vector.quantize_mx(T["qh" + name][:, 0:n], T["sh" + name][:, 0:n], T["h" + name][:, 0:4 * n]).then_inc(S["q" + name], 1)
+
+    relu_s("of", 0)
+    relu_s("of", 2)
+    g.scalar.wait_ge(S.pof, 1)
+    po = BANK * PB["of"]
+    g.scalar.activation(T.pof[:, oc:128], T.ps[:, po + oc:po + 128], ActivationFunctionType.Copy).then_inc(S.pofc, 1)
+    for b in (0, 2):
+        relu_s("f", b)
+    for b in (0, 2):
+        relu_s("l", b)
+    for b in range(G):
+        relu_s("ol", b)
+
+    Y = (T.y0, T.y1)
+    om = off[me]
+    nz = 0
+    for t, a, b in ((T.y0, om[3], om[4]), (T.y0, om[7], NC), (T.y1, om[1], om[2]), (T.y1, om[5], om[6])):
+        if b > a:
+            g.vector.memset(t[:, a:b], 0.0).then_inc(S.mz, 1)
+            nz += 1
+    g.vector.wait_ge(S.lx, nlx)
+    g.vector.quantize_mx(T.qx[:, 0:E], T.sx[:, 0:E], T.xt[:, 0:4 * E]).then_inc(S.qx_, 1)
+    g.vector.wait_ge(S.lw1a, 16)
+    g.vector.quantize_mx(T.qw0[:, 0:256], T.sw0[:, 0:256], T.w1t[:, 0:1024]).then_inc(S.qwa, 1)
+    g.vector.wait_ge(S.lw1b, 16)
+    g.vector.quantize_mx(T.qw0[:, 256:512], T.sw0[:, 256:512], T.w1t[:, 1024:2048]).then_inc(S.qwb, 1)
+    g.vector.wait_ge(S.lw2, 16)
+    g.vector.quantize_mx(T.qw0[:, 512:640], T.sw0[:, 512:640], T.w2t[:]).then_inc(S.qw2, 1)
+    for name in ("of", "f", "l"):
+        relu_v(name, 1)
+        relu_v(name, 3)
+        quant(name)
+
+    def gate(s):
+        a, b, cc = abc(s, k)
+        ga, gh = grow[s]
+        if p == 0:
+            return (0, a, ga), (a, b, ga + a), (a, b + cc, gh)
+        return (a + b, cc, gh + b), (a, b, gh), (0, a + b, ga)
+
+    def mul(out, o, in_, i, part, sem):
+        at, n, gcol = part
+        if n:
+            g.vector.tensor_tensor(out[:, o + at:o + at + n], in_[:, i + at:i + at + n], T.gb[:, gcol:gcol + n], AluOpType.mult).then_inc(sem, 1)
+        return 1 if n else 0
+
+    def join(out, o, in_, i, part, sem):
+        at, n, _ = part
+        if n:
+            v = out[:, o + at:o + at + n]
+            g.vector.tensor_tensor(v, v, in_[:, i + at:i + at + n], AluOpType.add).then_inc(sem, 1)
+        return 1 if n else 0
+
+    g.vector.wait_ge(S.gbd, 1)
+    g.vector.wait_ge(S.pf, 1)
+    order = sorted(srcs, key=lambda s: -sum(abc(s, k)))
+    ntf = 0
+    for s in order:
+        one, two, _ = gate(s)
+        pf = BANK * PB["f"] + land[s] - wf[0]
+        ntf += mul(T.res, land[s], T.ps, pf, one, S.tf)
+        ntf += mul(T.two, land[s], T.ps, pf, two, S.tf)
+    g.vector.wait_ge(S.pl, 1)
+    need = []
+    for i, s in enumerate(order):
+        need.append(["m%d" % i] if mul(T.res, land[s], T.ps, BANK * PB["l"] + land[s] - wl[0], gate(s)[2], S["m%d" % i]) else [])
+    g.vector.wait_ge(S.tf, ntf)
+    for i, s in enumerate(order):
+        if gate(s)[1][1]:
+            g.vector.wait_ge(S["m%d" % i], 1)
+            join(T.res, land[s], T.two, land[s], gate(s)[1], S["o%d" % i])
+            need[i].append("o%d" % i)
+
+    g.wait_ge(S.tf, ntf)
+    for i, s in enumerate(order):
+        for e in need[i]:
+            g.wait_ge(S[e], 1)
+        n = sum(abc(s, k))
+        d = off[s][lo]
+        put(s, Y[k % 2][:, d:d + n], T.res[:, land[s]:land[s] + n], S.ra, far)
+    g.wait_ge(S.ls, sent[0])
+
+    quant("ol")
+    one, two, lst = gate(me)
+    yo, own = om[lo], Y[k % 2]
+    g.vector.wait_ge(S.pofc, 1)
+    nto = mul(own, yo, T.pof, oc, one, S.to) + mul(T.two, LD, T.pof, oc, two, S.to)
+    g.vector.wait_ge(S.pol, 1)
+    if mul(own, yo, T.ps, BANK * PB["ol"] + oc, lst, S.mo):
+        g.vector.wait_ge(S.mo, 1)
+    if nto:
+        g.vector.wait_ge(S.to, nto)
+    if join(own, yo, T.two, LD, two, S.outo):
+        g.vector.wait_ge(S.outo, 1)
+
+    if nz:
+        g.vector.wait_ge(S.mz, nz)
+    g.vector.wait_ge(S.ra, 3 * bits(far))
+    w = om[1]
+    if w:
+        g.vector.tensor_tensor(T.yf[:, 0:w], T.y0[:, 0:w], T.y1[:, NC:NC + w], AluOpType.add).then_inc(S.add, 1)
+    g.vector.tensor_tensor(T.yf[:, w:NC], T.y0[:, w:NC], T.y1[:, w:NC], AluOpType.add).then_inc(S.add, 1)
+    g.sync.wait_ge(S.add, 2 if w else 1)
+    g.sync.dma_start(T.y[:], T.yf[:]).then_inc(S.yd, 16)
+    g.sync.wait_ge(S.yd, 16)

@@ -23,11 +23,10 @@ SCRATCH = {
     "two": ("sbuf", [128, LD + 128], "float32"),
     "gst": ("dram", [128, 4], "bfloat16"),
     "gl": ("dram", [3, 128, 4], "bfloat16"),
-    "grow": ("sbuf", [128, 640], "bfloat16"),
-    "gb": ("sbuf", [128, 640], "bfloat16"),
+    "grow": ("sbuf", [128, 800], "bfloat16"),
+    "gb": ("sbuf", [128, 800], "bfloat16"),
     "y0": ("sbuf", [128, NC + 128], "float32"),
     "y1": ("sbuf", [128, NC + 128], "float32"),
-    "yf": ("sbuf", [128, NC], "float32"),
     "ps": ("psum", [128, 4096], "float32"),
 }
 PASS = ("of", "f", "l", "ol")
@@ -35,8 +34,8 @@ for _n, _w in zip(PASS, (128, LD, LD, 128)):
     SCRATCH["h" + _n] = ("sbuf", [128, 4 * _w], "bfloat16")
     SCRATCH["qh" + _n] = ("sbuf", [128, _w], "float8_e4m3fn_x4")
     SCRATCH["sh" + _n] = ("sbuf", [128, _w], "uint8")
-SEMAPHORES = (["lx", "lg", "lw1a", "lw1b", "lw2", "mz", "qx_", "qwa", "qwb", "qw2", "ga", "gr", "gbd", "xa", "wa", "ra", "ls",
-               "add", "yd", "pofc", "tf", "to", "outo", "mo"]
+SEMAPHORES = (["lx", "lg", "lw1a", "lw1b", "lw2", "qx_", "qwa", "qwb", "qw2", "ga", "gr", "gbd", "xa", "wa", "ra", "ls",
+               "add", "cpy", "yd", "pofc", "tf", "to", "outo", "mo"]
               + [c + n + str(b) for c in "zr" for n in PASS for b in range(G)] + [c + n for c in "qp" for n in PASS]
               + [c + str(s) for c in "mo" for s in range(3)])
 
@@ -76,24 +75,36 @@ def rank_program(g, core, T, topo):
             start[m] = pos[(grp[m][0] - s0) % N]
         return s0, pos[-1], start
 
-    def sources(r):
-        k, p = place(r)
-        o = [grp[m][p] for m in range(K) if m != k]
+    def lineup(o, k):
         tot = sum(sum(abc(s, k)) for s in o)
         best = None
         for i in range(3):
             for l in range(3):
-                if i != l and tot - abc(o[i], k)[0] >= 128 and tot - abc(o[l], k)[2] >= 128:
-                    v = abc(o[i], k)[0] + abc(o[l], k)[2]
-                    if best is None or v > best[0]:
-                        best = (v, [o[i], o[3 - i - l], o[l]])
+                if i != l:
+                    a, c = tot - abc(o[i], k)[0], tot - abc(o[l], k)[2]
+                    if a >= 128 and c >= 128 and (best is None or a + c < best[0]):
+                        best = (a + c, [o[i], o[3 - i - l], o[l]])
+        return best
+
+    def share(k):
+        rs = [r for r in range(N) if r not in grp[k]]
+        best = None
+        for m in range(1 << len(rs)):
+            u = [r for i, r in enumerate(rs) if m >> i & 1]
+            v = [r for r in rs if r not in u]
+            if len(u) == 3:
+                a, b = lineup(u, k), lineup(v, k)
+                if a and b and (best is None or (max(a[0], b[0]), a[0] + b[0]) < best[0]):
+                    best = ((max(a[0], b[0]), a[0] + b[0]), (a[1], b[1]))
         return best[1]
 
+    shares = [share(k) for k in range(K)]
+
     def landing(r):
-        k, _ = place(r)
+        k, p = place(r)
         c = 0
         out = {}
-        for s in sources(r):
+        for s in shares[k][p]:
             out[s] = c
             c += sum(abc(s, k))
         return out, c
@@ -101,8 +112,11 @@ def rank_program(g, core, T, topo):
     k, p = place(me)
     lo, hi = grp[k]
     mate = grp[k][1 - p]
-    peers = [grp[(k + d) % K][p] for d in range(1, K)]
-    srcs = sources(me)
+    srcs = shares[k][p]
+    peers = []
+    for d in range(1, K):
+        m = (k + d) % K
+        peers.append(grp[m][0] if me in shares[m][0] else grp[m][1])
     land, end = landing(me)
     s0, E, start = xplan(me)
     far = topo.mask(core, T.cores[peers[0]])
@@ -125,11 +139,11 @@ def rank_program(g, core, T, topo):
     gr0 = 2 * NC // 4
     g.scalar.dma_start(T.gst[0:gr0, :], T.gt[:]).then_inc(S.lg, 16)
     g.sync.dma_start(T.xt[:, 0:4 * n1], T.x[:, 4 * off[me][s0]:4 * NC]).then_inc(S.lx, 16)
+    g.sync.dma_start(T.gst[gr0:128, :], T.gt[0:1, 0:4 * (128 - gr0)]).then_inc(S.lg, 16)
     nlx = 16
     if E > n1:
         g.scalar.dma_start(T.xt[:, 4 * n1:4 * E], T.x[:, 0:4 * (E - n1)]).then_inc(S.lx, 16)
         nlx = 32
-    g.scalar.dma_start(T.gst[gr0:128, :], T.gt[0:1, 0:4 * (128 - gr0)]).then_inc(S.lg, 16)
     g.sync.dma_start(T.w1t[:, 0:1024], T.w1[:, 0:1024]).then_inc(S.lw1a, 16)
     g.scalar.dma_start(T.w1t[:, 1024:2048], T.w1[:, 1024:2048]).then_inc(S.lw1b, 16)
     g.sync.dma_start(T.w2t[:], T.w2[:]).then_inc(S.lw2, 16)
@@ -160,8 +174,9 @@ def rank_program(g, core, T, topo):
     ids, dsts = [], []
     for q in peers:
         rid, pid, _ = topo.addr(T.cores[q])
+        kq, pq = place(q)
         ids.append(DstId(rid=rid, pnc=pid))
-        dsts.append(T.gl[sources(q).index(me)])
+        dsts.append(T.gl[shares[kq][pq].index(me)])
     g.remote_dma_fused([RemoteDMATransfer(dst_ids=ids, dma_engine_mask=far, remote_sem=S.ga,
                                           srcs=[T.gst[:]], dsts=dsts, alu_op=0)], local_sem=S.ls)
     sent[0] += bits(far)
@@ -257,11 +272,6 @@ def rank_program(g, core, T, topo):
 
     Y = (T.y0, T.y1)
     om = off[me]
-    nz = 0
-    for t, a, b in ((T.y0, om[3], om[4]), (T.y0, om[7], NC), (T.y1, om[1], om[2]), (T.y1, om[5], om[6])):
-        if b > a:
-            g.vector.memset(t[:, a:b], 0.0).then_inc(S.mz, 1)
-            nz += 1
     g.vector.wait_ge(S.lx, nlx)
     g.vector.quantize_mx(T.qx[:, 0:E], T.sx[:, 0:E], T.xt[:, 0:4 * E]).then_inc(S.qx_, 1)
     g.vector.wait_ge(S.lw1a, 16)
@@ -305,15 +315,27 @@ def rank_program(g, core, T, topo):
         ntf += mul(T.res, land[s], T.ps, pf, one, S.tf)
         ntf += mul(T.two, land[s], T.ps, pf, two, S.tf)
     g.vector.wait_ge(S.pl, 1)
-    need = []
-    for i, s in enumerate(order):
-        need.append(["m%d" % i] if mul(T.res, land[s], T.ps, BANK * PB["l"] + land[s] - wl[0], gate(s)[2], S["m%d" % i]) else [])
-    g.vector.wait_ge(S.tf, ntf)
-    for i, s in enumerate(order):
+    need = [[], [], []]
+
+    def last_mul(i):
+        s = order[i]
+        if mul(T.res, land[s], T.ps, BANK * PB["l"] + land[s] - wl[0], gate(s)[2], S["m%d" % i]):
+            need[i].append("m%d" % i)
+
+    def last_add(i):
+        s = order[i]
         if gate(s)[1][1]:
             g.vector.wait_ge(S["m%d" % i], 1)
             join(T.res, land[s], T.two, land[s], gate(s)[1], S["o%d" % i])
             need[i].append("o%d" % i)
+
+    last_mul(0)
+    last_mul(1)
+    g.vector.wait_ge(S.tf, ntf)
+    last_add(0)
+    last_mul(2)
+    last_add(1)
+    last_add(2)
 
     g.wait_ge(S.tf, ntf)
     for i, s in enumerate(order):
@@ -336,14 +358,24 @@ def rank_program(g, core, T, topo):
         g.vector.wait_ge(S.to, nto)
     if join(own, yo, T.two, LD, two, S.outo):
         g.vector.wait_ge(S.outo, 1)
+        if k % 2:
+            g.scalar.wait_ge(S.outo, 1)
 
-    if nz:
-        g.vector.wait_ge(S.mz, nz)
     g.vector.wait_ge(S.ra, 3 * bits(far))
-    w = om[1]
-    if w:
-        g.vector.tensor_tensor(T.yf[:, 0:w], T.y0[:, 0:w], T.y1[:, NC:NC + w], AluOpType.add).then_inc(S.add, 1)
-    g.vector.tensor_tensor(T.yf[:, w:NC], T.y0[:, w:NC], T.y1[:, w:NC], AluOpType.add).then_inc(S.add, 1)
-    g.sync.wait_ge(S.add, 2 if w else 1)
-    g.sync.dma_start(T.y[:], T.yf[:]).then_inc(S.yd, 16)
+    g.scalar.wait_ge(S.ra, 3 * bits(far))
+    na = nc = 0
+    for e in range(N):
+        u, n = om[e], cnt[me][e]
+        if n and e % 2 == 0:
+            w = u if e else NC
+            g.vector.tensor_tensor(T.y0[:, u:u + n], T.y0[:, u:u + n], T.y1[:, w:w + n], AluOpType.add).then_inc(S.add, 1)
+            na += 1
+        elif n and (e // 2) % 2:
+            g.scalar.activation(T.y0[:, u:u + n], T.y1[:, u:u + n], ActivationFunctionType.Copy).then_inc(S.cpy, 1)
+            nc += 1
+    if na:
+        g.sync.wait_ge(S.add, na)
+    if nc:
+        g.sync.wait_ge(S.cpy, nc)
+    g.sync.dma_start(T.y[:], T.y0[:, 0:NC]).then_inc(S.yd, 16)
     g.sync.wait_ge(S.yd, 16)

from concourse.bass import DstId, RemoteDMATransfer
from concourse.mybir import dt, AluOpType, ActivationFunctionType

N, NC, G = 8, 192, 4
KC = 0.047
XE = 272
LD = 288

SCRATCH = {
    "xt": ("sbuf", [128, 4 * XE], "bfloat16"),
    "w1t": ("sbuf", [128, 2048], "bfloat16"),
    "w2t": ("sbuf", [128, 512], "bfloat16"),
    "qx": ("sbuf", [128, XE], "float8_e4m3fn_x4"),
    "sx": ("sbuf", [128, XE], "uint8"),
    "ql": ("sbuf", [128, LD], "float8_e4m3fn_x4"),
    "sl": ("sbuf", [128, LD], "uint8"),
    "qw0": ("sbuf", [128, 640], "float8_e4m3fn_x4"),
    "sw0": ("sbuf", [128, 640], "uint8"),
    "qw1": ("sbuf", [128, 640], "float8_e4m3fn_x4"),
    "sw1": ("sbuf", [128, 640], "uint8"),
    "pof": ("sbuf", [128, 128], "float32"),
    "res": ("sbuf", [128, LD], "float32"),
    "two": ("sbuf", [128, LD + 128], "float32"),
    "gst": ("dram", [128, 4], "bfloat16"),
    "gl": ("dram", [3, 128, 4], "bfloat16"),
    "grow": ("sbuf", [128, 800], "bfloat16"),
    "gb": ("sbuf", [128, 800], "bfloat16"),
    "y0": ("sbuf", [128, NC + 128], "float32"),
    "y1": ("sbuf", [128, NC + 128], "float32"),
    "ps": ("psum", [128, 4096], "float32"),
}
PASS = ("of", "f", "l", "ol")
for _n, _w in zip(PASS, (128, LD, LD, 128)):
    SCRATCH["h" + _n] = ("sbuf", [128, 4 * _w], "bfloat16")
    SCRATCH["qh" + _n] = ("sbuf", [128, _w], "float8_e4m3fn_x4")
    SCRATCH["sh" + _n] = ("sbuf", [128, _w], "uint8")
SEMAPHORES = (["lx", "lg", "lw1a", "lw1b", "lw2", "qx_", "qwa", "qwb", "qw2", "ga", "gr", "gbd", "xa", "wa", "ra", "ls",
               "add", "cpy", "yd", "pofc", "tf", "to", "outo", "mo"]
              + [c + n + str(b) for c in "zr" for n in PASS for b in range(G)] + [c + n for c in "qp" for n in PASS]
              + [c + str(s) for c in "mo" for s in range(3)])


def rank_program(g, core, T, topo):
    me = T.rank_of(core)
    if me is None:
        return
    S = T.sem
    cnt = T.tables["CNT"]
    off = [[sum(c[:e]) for e in range(N + 1)] for c in cnt]
    chips = []
    for r in range(N):
        c = topo.chip(T.cores[r])
        if c not in chips:
            chips.append(c)
    grp = [[r for r in range(N) if topo.chip(T.cores[r]) == c] for c in chips]
    K = len(grp)

    def place(r):
        for k in range(K):
            if r in grp[k]:
                return k, grp[k].index(r)

    def abc(j, k):
        lo, hi = grp[k]
        return cnt[j][lo], cnt[j][hi], cnt[j][(hi + 1) % N]

    def xplan(j):
        k, _ = place(j)
        s0 = (grp[k][1] + 1) % N
        pos = [0]
        for i in range(N + 1):
            pos.append(pos[-1] + cnt[j][(s0 + i) % N])
        start = {}
        for m in range(K):
            start[m] = pos[(grp[m][0] - s0) % N]
        return s0, pos[-1], start

    def lineup(o, k):
        tot = sum(sum(abc(s, k)) for s in o)
        best = None
        for i in range(3):
            for l in range(3):
                if i != l:
                    a, c = tot - abc(o[i], k)[0], tot - abc(o[l], k)[2]
                    if a >= 128 and c >= 128 and (best is None or a + c < best[0]):
                        best = (a + c, [o[i], o[3 - i - l], o[l]])
        return best

    def share(k):
        rs = [r for r in range(N) if r not in grp[k]]
        best = None
        for m in range(1 << len(rs)):
            u = [r for i, r in enumerate(rs) if m >> i & 1]
            v = [r for r in rs if r not in u]
            if len(u) == 3:
                a, b = lineup(u, k), lineup(v, k)
                if a and b and (best is None or (max(a[0], b[0]), a[0] + b[0]) < best[0]):
                    best = ((max(a[0], b[0]), a[0] + b[0]), (a[1], b[1]))
        return best[1]

    shares = [share(k) for k in range(K)]

    def landing(r):
        k, p = place(r)
        c = 0
        out = {}
        for s in shares[k][p]:
            out[s] = c
            c += sum(abc(s, k))
        return out, c

    k, p = place(me)
    lo, hi = grp[k]
    mate = grp[k][1 - p]
    srcs = shares[k][p]
    peers = []
    for d in range(1, K):
        m = (k + d) % K
        peers.append(grp[m][0] if me in shares[m][0] else grp[m][1])
    land, end = landing(me)
    s0, E, start = xplan(me)
    far = topo.mask(core, T.cores[peers[0]])
    near = topo.mask(core, T.cores[mate])
    for q in peers:
        far = far & topo.mask(core, T.cores[q])
    near = near & ~far

    def bits(m):
        return bin(m).count("1")

    sent = [0]

    def put(dst, out, in_, sem, mask):
        rid, pid, _ = topo.addr(T.cores[dst])
        g.remote_dma(out, in_, sem, S.ls, pid, rid, mask)
        sent[0] += bits(mask)

    n1 = NC - off[me][s0]
    gr0 = 2 * NC // 4
    g.scalar.dma_start(T.gst[0:gr0, :], T.gt[:]).then_inc(S.lg, 16)
    g.sync.dma_start(T.xt[:, 0:4 * n1], T.x[:, 4 * off[me][s0]:4 * NC]).then_inc(S.lx, 16)
    g.sync.dma_start(T.gst[gr0:128, :], T.gt[0:1, 0:4 * (128 - gr0)]).then_inc(S.lg, 16)
    nlx = 16
    if E > n1:
        g.scalar.dma_start(T.xt[:, 4 * n1:4 * E], T.x[:, 0:4 * (E - n1)]).then_inc(S.lx, 16)
        nlx = 32
    g.sync.dma_start(T.w1t[:, 0:1024], T.w1[:, 0:1024]).then_inc(S.lw1a, 16)
    g.scalar.dma_start(T.w1t[:, 1024:2048], T.w1[:, 1024:2048]).then_inc(S.lw1b, 16)
    g.sync.dma_start(T.w2t[:], T.w2[:]).then_inc(S.lw2, 16)

    grow = {}
    c = 0
    loads = []
    for s in srcs + [me]:
        o = off[s]
        a, b, cc = abc(s, k)
        e2 = (hi + 1) % N
        grow[s] = (c, c + a + b)
        for row, at, n in ((0, o[lo], a), (1, o[hi], b), (0, o[hi], b), (1, o[e2], cc)):
            if n:
                loads.append((s, row, at, n, c))
            c += n
    ng = c
    for s, row, at, n, c in loads:
        if s == me:
            g.sync.dma_start(T.grow[0:1, c:c + n], T.gt[row:row + 1, at:at + n]).then_inc(S.gr, 16)
    g.sync.wait_ge(S.ga, 3 * bits(far))
    for s, row, at, n, c in loads:
        if s != me:
            r0 = (row * NC + at) // 4
            g.sync.dma_start(T.grow[0:1, c:c + n], T.gl[srcs.index(s)][r0:r0 + n // 4, :]).then_inc(S.gr, 16)

    g.wait_ge(S.lg, 32)
    ids, dsts = [], []
    for q in peers:
        rid, pid, _ = topo.addr(T.cores[q])
        kq, pq = place(q)
        ids.append(DstId(rid=rid, pnc=pid))
        dsts.append(T.gl[shares[kq][pq].index(me)])
    g.remote_dma_fused([RemoteDMATransfer(dst_ids=ids, dma_engine_mask=far, remote_sem=S.ga,
                                          srcs=[T.gst[:]], dsts=dsts, alu_op=0)], local_sem=S.ls)
    sent[0] += bits(far)
    g.wait_ge(S.qx_, 1)
    for q in peers:
        kq = place(q)[0]
        a, n = start[kq], sum(abc(me, kq))
        d = landing(q)[0][me]
        put(q, T.ql[:, d:d + n].bitcast(dt.uint8), T.qx[:, a:a + n].bitcast(dt.uint8), S.xa, far)
        put(q, T.sl[:, d:d + n], T.sx[:, a:a + n], S.xa, far)
    g.wait_ge(S.qwa, 1)
    g.wait_ge(S.qwb, 1)
    g.wait_ge(S.qw2, 1)
    put(mate, T.qw1[:].bitcast(dt.uint8), T.qw0[:].bitcast(dt.uint8), S.wa, near)
    put(mate, T.sw1[:], T.sw0[:], S.wa, near)
    g.wait_ge(S.gr, 16 * len(loads))
    g.partition_broadcast(T.gb[:, 0:ng], T.grow[0:1, 0:ng], 128).then_inc(S.gbd, 1)

    A0, C0 = abc(srcs[0], k)[0], abc(srcs[-1], k)[2]
    wlo, whi = (0, end - C0), (A0, end)
    wf, wl = (wlo, whi) if p == 0 else (whi, wlo)
    wo = (E - 128, E)
    no = sum(abc(me, k))
    oc = 128 - no
    wins = {"of": wo, "f": wf, "l": wl, "ol": wo}
    banks = {"of": (4, 5, 6, 7), "f": (0, 1, 2, 3), "l": (4, 5, 6, 7), "ol": (1, 2, 3, 5)}
    PB = {"of": 4, "f": 0, "l": 4, "ol": 6}
    BANK = 512

    def bank(b, n):
        return T.ps[:, BANK * b:BANK * b + n]

    def width(name):
        return wins[name][1] - wins[name][0]

    def zs(name, qw, sw, qm, sm):
        u, v = wins[name]
        for b in range(G):
            g.tensor.matmul_mx(bank(banks[name][b], v - u), qw[:, 128 * b:128 * b + 128], sw[:, 128 * b:128 * b + 128],
                               qm[:, u:v], sm[:, u:v], True, True).then_inc(S["z%s%d" % (name, b)], 1)

    def ptile(name, qw, sw):
        n = width(name)
        g.tensor.wait_ge(S["q" + name], 1)
        g.tensor.matmul_mx(bank(PB[name], n), qw[:, 512:640], sw[:, 512:640], T["qh" + name][:, 0:n], T["sh" + name][:, 0:n],
                           True, True).then_inc(S["p" + name], 1)

    g.tensor.wait_ge(S.qx_, 1)
    g.tensor.wait_ge(S.qwa, 1)
    g.tensor.wait_ge(S.qwb, 1)
    zs("of", T.qw0, T.sw0, T.qx, T.sx)
    g.tensor.wait_ge(S.qw2, 1)
    ptile("of", T.qw0, T.sw0)
    g.tensor.wait_ge(S.xa, 6 * bits(far))
    zs("f", T.qw0, T.sw0, T.ql, T.sl)
    g.tensor.wait_ge(S.wa, 2 * bits(near))
    g.tensor.wait_ge(S.pofc, 1)
    zs("l", T.qw1, T.sw1, T.ql, T.sl)
    ptile("f", T.qw0, T.sw0)
    ptile("l", T.qw1, T.sw1)
    zs("ol", T.qw1, T.sw1, T.qx, T.sx)
    ptile("ol", T.qw1, T.sw1)

    def relu_s(name, b):
        n = width(name)
        g.scalar.wait_ge(S["z%s%d" % (name, b)], 1)
        g.scalar.activation(T["h" + name][:, b:4 * n:4], bank(banks[name][b], n), ActivationFunctionType.Relu,
                            scale=KC).then_inc(S["r%s%d" % (name, b)], 1)

    def relu_v(name, b):
        n = width(name)
        g.vector.wait_ge(S["z%s%d" % (name, b)], 1)
        g.vector.tensor_scalar(T["h" + name][:, b:4 * n:4], bank(banks[name][b], n), 0.0, KC, AluOpType.max,
                               AluOpType.mult).then_inc(S["r%s%d" % (name, b)], 1)

    def quant(name):
        n = width(name)
        for b in range(G):
            g.vector.wait_ge(S["r%s%d" % (name, b)], 1)
        g.vector.quantize_mx(T["qh" + name][:, 0:n], T["sh" + name][:, 0:n], T["h" + name][:, 0:4 * n]).then_inc(S["q" + name], 1)

    relu_s("of", 0)
    relu_s("of", 2)
    g.scalar.wait_ge(S.pof, 1)
    po = BANK * PB["of"]
    g.scalar.activation(T.pof[:, oc:128], T.ps[:, po + oc:po + 128], ActivationFunctionType.Copy).then_inc(S.pofc, 1)
    for b in (0, 2):
        relu_s("f", b)
    for b in (0, 2):
        relu_s("l", b)
    for b in range(G):
        relu_s("ol", b)

    Y = (T.y0, T.y1)
    om = off[me]
    g.vector.wait_ge(S.lx, nlx)
    g.vector.quantize_mx(T.qx[:, 0:E], T.sx[:, 0:E], T.xt[:, 0:4 * E]).then_inc(S.qx_, 1)
    g.vector.wait_ge(S.lw1a, 16)
    g.vector.quantize_mx(T.qw0[:, 0:256], T.sw0[:, 0:256], T.w1t[:, 0:1024]).then_inc(S.qwa, 1)
    g.vector.wait_ge(S.lw1b, 16)
    g.vector.quantize_mx(T.qw0[:, 256:512], T.sw0[:, 256:512], T.w1t[:, 1024:2048]).then_inc(S.qwb, 1)
    g.vector.wait_ge(S.lw2, 16)
    g.vector.quantize_mx(T.qw0[:, 512:640], T.sw0[:, 512:640], T.w2t[:]).then_inc(S.qw2, 1)
    for name in ("of", "f", "l"):
        relu_v(name, 1)
        relu_v(name, 3)
        quant(name)

    def gate(s):
        a, b, cc = abc(s, k)
        ga, gh = grow[s]
        if p == 0:
            return (0, a, ga), (a, b, ga + a), (a, b + cc, gh)
        return (a + b, cc, gh + b), (a, b, gh), (0, a + b, ga)

    def mul(out, o, in_, i, part, sem):
        at, n, gcol = part
        if n:
            g.vector.tensor_tensor(out[:, o + at:o + at + n], in_[:, i + at:i + at + n], T.gb[:, gcol:gcol + n], AluOpType.mult).then_inc(sem, 1)
        return 1 if n else 0

    def join(out, o, in_, i, part, sem):
        at, n, _ = part
        if n:
            v = out[:, o + at:o + at + n]
            g.vector.tensor_tensor(v, v, in_[:, i + at:i + at + n], AluOpType.add).then_inc(sem, 1)
        return 1 if n else 0

    g.vector.wait_ge(S.gbd, 1)
    g.vector.wait_ge(S.pf, 1)
    order = sorted(srcs, key=lambda s: -sum(abc(s, k)))
    ntf = 0
    for s in order:
        one, two, _ = gate(s)
        pf = BANK * PB["f"] + land[s] - wf[0]
        ntf += mul(T.res, land[s], T.ps, pf, one, S.tf)
        ntf += mul(T.two, land[s], T.ps, pf, two, S.tf)
    g.vector.wait_ge(S.pl, 1)
    need = [[], [], []]

    def last_mul(i):
        s = order[i]
        if mul(T.res, land[s], T.ps, BANK * PB["l"] + land[s] - wl[0], gate(s)[2], S["m%d" % i]):
            need[i].append("m%d" % i)

    def last_add(i):
        s = order[i]
        if gate(s)[1][1]:
            g.vector.wait_ge(S["m%d" % i], 1)
            join(T.res, land[s], T.two, land[s], gate(s)[1], S["o%d" % i])
            need[i].append("o%d" % i)

    last_mul(0)
    last_mul(1)
    g.vector.wait_ge(S.tf, ntf)
    last_add(0)
    last_mul(2)
    last_add(1)
    last_add(2)

    g.wait_ge(S.tf, ntf)
    for i, s in enumerate(order):
        for e in need[i]:
            g.wait_ge(S[e], 1)
        n = sum(abc(s, k))
        d = off[s][lo]
        put(s, Y[k % 2][:, d:d + n], T.res[:, land[s]:land[s] + n], S.ra, far)
    g.wait_ge(S.ls, sent[0])

    quant("ol")
    one, two, lst = gate(me)
    yo, own = om[lo], Y[k % 2]
    g.vector.wait_ge(S.pofc, 1)
    nto = mul(own, yo, T.pof, oc, one, S.to) + mul(T.two, LD, T.pof, oc, two, S.to)
    g.vector.wait_ge(S.pol, 1)
    if mul(own, yo, T.ps, BANK * PB["ol"] + oc, lst, S.mo):
        g.vector.wait_ge(S.mo, 1)
    if nto:
        g.vector.wait_ge(S.to, nto)
    if join(own, yo, T.two, LD, two, S.outo):
        g.vector.wait_ge(S.outo, 1)
        if k % 2:
            g.scalar.wait_ge(S.outo, 1)

    g.vector.wait_ge(S.ra, 3 * bits(far))
    g.scalar.wait_ge(S.ra, 3 * bits(far))
    na = nc = 0
    for e in range(N):
        u, n = om[e], cnt[me][e]
        if n and e % 2 == 0:
            w = u if e else NC
            g.vector.tensor_tensor(T.y0[:, u:u + n], T.y0[:, u:u + n], T.y1[:, w:w + n], AluOpType.add).then_inc(S.add, 1)
            na += 1
        elif n and (e // 2) % 2:
            g.scalar.activation(T.y0[:, u:u + n], T.y1[:, u:u + n], ActivationFunctionType.Copy).then_inc(S.cpy, 1)
            nc += 1
    if na:
        g.sync.wait_ge(S.add, na)
    if nc:
        g.sync.wait_ge(S.cpy, nc)
    g.sync.dma_start(T.y[:], T.y0[:, 0:NC]).then_inc(S.yd, 16)
    g.sync.wait_ge(S.yd, 16)
